import numpy as np
import ml_dtypes


def mxq(x, axis, fmt="e4m3"):
    dtype, down = {"e4m3": (ml_dtypes.float8_e4m3fn, 7), "e5m2": (ml_dtypes.float8_e5m2, 14)}[fmt]
    v = np.moveaxis(np.asarray(x, np.float32).astype(ml_dtypes.bfloat16).astype(np.float64), axis, -1)
    blocks = v.reshape(v.shape[:-1] + (-1, 32))
    amax = np.abs(blocks).max(-1, keepdims=True)
    byte = np.maximum(np.where(amax > 0, np.frexp(amax)[1] - 1 + 127, 0) - down, 1)
    scale = np.exp2(byte - 127.0)
    codes = (blocks / scale).astype(np.float32).astype(dtype).astype(np.float64)
    return np.moveaxis((codes * scale).reshape(v.shape), -1, axis)


WIDE = False


def mx_kscale(k):
    if not WIDE:
        return np.ones(k)
    levels = np.array([10, -10, 5, -5, 0])
    if k % 512:
        return np.exp2(np.random.permutation(np.resize(levels, k // 32))).repeat(32)
    a = np.empty((k // 512, 16))
    for p in range(k // 512):
        a[p, :8] = np.random.permutation(np.resize(levels, 8))
        for g in range(8):
            far = levels[np.abs(levels - a[p, g]) >= 10]
            a[p, g + 8] = far[np.random.randint(len(far))]
    return np.exp2(a.ravel()).repeat(32)


def f64(x):
    return np.asarray(x).astype(np.float64)


def striped(idx):
    return np.tile(idx.reshape(-1, 16).T, (8, 1)).astype(np.uint16)


def unstriped(offs):
    return offs[:16].T.reshape(-1).astype(np.int64)


E2M1 = np.array([0.0, 0.5, 1.0, 1.5, 2.0, 3.0, 4.0, 6.0, -0.0, -0.5, -1.0, -1.5, -2.0, -3.0, -4.0, -6.0])


def pack_weight(w, fmt):
    k, n = w.shape
    w = f64(np.asarray(w, np.float32).astype(ml_dtypes.bfloat16)).reshape(k // 32, 32, n)
    amax = np.abs(w).max(1)
    if fmt == "e4m3":
        byte = np.frexp(amax)[1] - 1 + 127 - 7
    else:
        mant, ex = np.frexp(amax / 6.0)
        byte = np.where(mant > 0.5, ex, ex - 1) + 127
    byte = np.clip(np.where(amax > 0, byte, 1), 1, 254)
    scaled = (w * np.exp2(127.0 - byte)[:, None, :]).reshape(k, n).astype(np.float32)
    by_word = np.ascontiguousarray(scaled.reshape(k // 512, 128, 4, n).transpose(0, 1, 3, 2))
    if fmt == "e4m3":
        words = by_word.astype(ml_dtypes.float8_e4m3fn).view(np.uint8)
    else:
        c = by_word.astype(ml_dtypes.float4_e2m1fn).view(np.uint8) & 0xF
        words = (c[..., 0::2] | (c[..., 1::2] << 4)).reshape(k // 512, 128, 2 * n)
    return np.ascontiguousarray(words), np.ascontiguousarray(byte.astype(np.uint8).reshape(k // 512, 16, n))


def unpack_weight(words, scales, fmt):
    g, _, n = scales.shape
    words = np.ascontiguousarray(words).reshape(g, 128, n, -1)
    if fmt == "e4m3":
        vals = words.view(ml_dtypes.float8_e4m3fn).astype(np.float64)
    else:
        nib = np.empty((g, 128, n, 4), np.uint8)
        nib[..., 0::2] = words & 0xF
        nib[..., 1::2] = words >> 4
        vals = E2M1[nib]
    vals = vals * np.repeat(np.exp2(scales.astype(np.float64) - 127.0), 8, axis=1)[..., None]
    return vals.transpose(0, 1, 3, 2).reshape(g * 512, n)


def pack_table(v):
    words, scales = pack_weight(v, "e4m3")
    return np.concatenate([words.reshape(words.shape[0], -1), scales.reshape(scales.shape[0], -1)], axis=1)


def unpack_table(tab):
    g, t = tab.shape[0], tab.shape[1] // 528
    return unpack_weight(tab[:, :512 * t].reshape(g, 128, t, 4), tab[:, 512 * t:].reshape(g, 16, t), "e4m3")


K, M, T, S = 1536, 256, 1024, 512


def setup_inputs():
    n = np.random.standard_normal
    s = mx_kscale(K)[:, None]
    return {
        "tab": pack_table(n((K, T)) * s),
        "w": (n((K, M)) / np.sqrt(K) / s).astype(np.float32),
        "b": (0.3 * n(256)).astype(np.float32),
        "wgo": np.tile(np.random.uniform(0.5, 2.0, S), (128, 1)).astype(np.float32),
        "offs": striped(np.random.permutation(T)[:S]),
        "offs2": striped(np.random.permutation(T)[:S]),
    }


def reference(tab, w, b, wgo, offs, offs2):
    tab_ = unpack_table(tab)[:, unstriped(offs)]
    w_ = mxq(f64(w), 0, "e4m3")
    y = w_.T @ tab_
    out = np.zeros((M, T))
    out[:, unstriped(offs2)] = f64(wgo)[0] * (y + f64(b)[:, None])
    return out

@@ -1,0 +1,142 @@
+from contextlib import ExitStack
+
+import concourse.mybir as mybir
+
+K, M, T, S = 1536, 256, 1024, 512
+FLOPS = 2 * K * M * S
+
+F32 = mybir.dt.float32
+BF16 = mybir.dt.bfloat16
+I32 = mybir.dt.int32
+U32 = mybir.dt.uint32
+U16 = mybir.dt.uint16
+U8 = mybir.dt.uint8
+FP8X4 = mybir.dt.float8_e4m3fn_x4
+MULT = mybir.AluOpType.mult
+IDENT = mybir.ActivationFunctionType.Identity
+
+P = 128
+PASSES = K // 512
+HALVES = M // 128
+PIECES = 2
+PIECE = S // PIECES
+
+
+def tile_list_tabscat_bias_kernel(tc, tab, w, b, wgo, offs, offs2, out):
+    nc = tc.nc
+    with ExitStack() as ctx:
+        lists = ctx.enter_context(tc.tile_pool(name="lists", bufs=1))
+        keep = ctx.enter_context(tc.tile_pool(name="keep", bufs=1))
+        psum = ctx.enter_context(tc.psum_pool(name="psum", bufs=1))
+
+        offs_sb = lists.tile([P, S // 16], U16, name="offs_sb")
+        offs2_sb = lists.tile([P, S // 16], U16, name="offs2_sb")
+
+        scale_tab = keep.tile([P, T // 4], I32, name="scale_tab", align_bytes=64)
+        nc.vector.memset(scale_tab[:], 0)
+
+        nc.sync.dma_start(offs_sb[:], offs)
+        tab_words = [keep.tile([P, T], I32, name=f"tab_words{a}", align_bytes=64) for a in range(PASSES)]
+        w_raw = [keep.tile([P, 4, M], F32, name=f"w_raw{a}", align_bytes=64) for a in range(PASSES)]
+
+        def load_tab(a):
+            nc.sync.dma_start(tab_words[a][:], tab[a, 0 : 512 * T].rearrange("(p x) -> p x", p=P).bitcast(I32))
+
+        def load_w(a):
+            nc.sync.dma_start(w_raw[a][:], w[512 * a : 512 * (a + 1), :].rearrange("(p j) n -> p j n", j=4))
+
+        def load_scales(queue, q):
+            queue.dma_start(
+                scale_tab[32 * q : 32 * q + 12, :],
+                tab[:, 512 * T + 4 * T * q : 512 * T + 4 * T * (q + 1)].rearrange("a (r t) -> a r t", r=4).bitcast(I32),
+            )
+
+        load_tab(0)
+        bias = [keep.tile([P, 1], F32, name=f"bias{h}") for h in range(HALVES)]
+        for h in range(HALVES):
+            nc.gpsimd.dma_start(bias[h][:], b[128 * h : 128 * (h + 1)].unsqueeze(1))
+        load_scales(nc.scalar, 0)
+        load_scales(nc.scalar, 1)
+        load_w(0)
+        load_scales(nc.sync, 2)
+        load_scales(nc.sync, 3)
+        load_tab(1)
+        load_w(1)
+        load_w(2)
+        load_tab(2)
+        nc.sync.dma_start(offs2_sb[:], offs2)
+        wgo_sb = keep.tile([P, S], F32, name="wgo_sb")
+        nc.sync.dma_start(wgo_sb[:], wgo)
+
+        warm = keep.tile([P, 1], F32, name="warm")
+        nc.vector.memset(warm[:], 0.0)
+        nc.scalar.activation(warm[:], warm[:], IDENT)
+
+        placed = [keep.tile([P, T], F32, name=f"placed{h}") for h in range(HALVES)]
+        for h in range(HALVES):
+            nc.vector.memset(placed[h][:], 0.0)
+
+        words = [keep.tile([P, S], U32, name=f"words{a}", align_bytes=64) for a in range(PASSES)]
+        scales = keep.tile([P, S], U8, name="scales", align_bytes=64)
+        w_bf = [keep.tile([P, M, 4], BF16, name=f"w_bf{a}", align_bytes=64) for a in range(2)]
+        w_bf_last = [keep.tile([P, 128, 4], BF16, name=f"w_bf_last{h}", align_bytes=64) for h in range(HALVES)]
+        w_words = [keep.tile([P, M], U32, name=f"w_words{a}", align_bytes=64) for a in range(PASSES)]
+        w_scales = [keep.tile([P, M], U8, name=f"w_scales{a}", align_bytes=64) for a in range(PASSES)]
+        acc0 = [psum.tile([P, PIECE], F32, name=f"acc0{c}") for c in range(PIECES)]
+        acc1 = psum.tile([P, S], F32, name="acc1")
+        y0 = [keep.tile([P, PIECE], F32, name=f"y0{c}") for c in range(PIECES)]
+        y1 = keep.tile([P, S], F32, name="y1")
+
+        def gather_words(a, first=0, end=S):
+            nc.vector.tensor_copy(words[a][:, first:end], tab_words[a][:].bitcast(U32).indirect(offs_sb[:, first // 16 : end // 16]))
+
+        def quantise_w(a, cols, rounded):
+            nc.scalar.copy(
+                rounded.rearrange("p (c i) j -> p c j i", i=4),
+                w_raw[a][:, :, cols].rearrange("p j (c i) -> p c j i", i=4),
+            )
+            nc.vector.quantize_mx(w_words[a][:, cols].bitcast(FP8X4), w_scales[a][:, cols], rounded.rearrange("p n j -> p (n j)"))
+
+        def multiply(acc, a, h, cols):
+            rows = slice(128 * h, 128 * (h + 1))
+            nc.tensor.matmul_mx(
+                acc[:],
+                lhsT=w_words[a][:, rows].bitcast(FP8X4),
+                lhsT_scale=w_scales[a][:, rows],
+                rhs=words[a][:, cols].bitcast(FP8X4),
+                rhs_scale=scales[4 * a : P, cols],
+                start=(a == 0),
+                stop=(a == PASSES - 1),
+            )
+
+        def scatter(h, values, first, count):
+            nc.vector.tensor_tensor(
+                placed[h][:].indirect(offs2_sb[:, first // 16 : (first + count) // 16]),
+                values,
+                wgo_sb[:, first : first + count],
+                MULT,
+            )
+
+        pieces = [slice(PIECE * c, PIECE * (c + 1)) for c in range(PIECES)]
+        gather_words(0)
+        nc.vector.tensor_copy(scales[:], scale_tab[:].bitcast(U8).indirect(offs_sb[:]))
+        gather_words(1)
+        for a in range(2):
+            quantise_w(a, slice(0, M), w_bf[a][:])
+        for h in range(HALVES):
+            quantise_w(2, slice(128 * h, 128 * (h + 1)), w_bf_last[h][:])
+        for a in range(2):
+            for c in range(PIECES):
+                multiply(acc0[c], a, 0, pieces[c])
+        for c in range(PIECES):
+            gather_words(2, PIECE * c, PIECE * (c + 1))
+            multiply(acc0[c], 2, 0, pieces[c])
+            nc.scalar.activation(y0[c][:], acc0[c][:], IDENT, bias=bias[0][:])
+        for a in range(PASSES):
+            multiply(acc1, a, 1, slice(0, S))
+        nc.scalar.activation(y1[:], acc1[:], IDENT, bias=bias[1][:])
+        for c in range(PIECES):
+            scatter(0, y0[c][:], PIECE * c, PIECE)
+        nc.sync.dma_start(out[0:P, :], placed[0][:])
+        scatter(1, y1[:], 0, S)
+        nc.sync.dma_start(out[P : 2 * P, :], placed[1][:])

@@ -18,8 +18,8 @@ IDENT = mybir.ActivationFunctionType.Identity
 P = 128
 PASSES = K // 512
 HALVES = M // 128
-PIECES = 2
-PIECE = S // PIECES
+CUTS = [0, 128, S]
+PIECES = len(CUTS) - 1
 
 
 def tile_list_tabscat_bias_kernel(tc, tab, w, b, wgo, offs, offs2, out):
@@ -33,11 +33,12 @@ def tile_list_tabscat_bias_kernel(tc, tab, w, b, wgo, offs, offs2, out):
         offs2_sb = lists.tile([P, S // 16], U16, name="offs2_sb")
 
         scale_tab = keep.tile([P, T // 4], I32, name="scale_tab", align_bytes=64)
-        nc.vector.memset(scale_tab[:], 0)
+        nc.gpsimd.memset(scale_tab[:], 0)
 
-        nc.sync.dma_start(offs_sb[:], offs)
         tab_words = [keep.tile([P, T], I32, name=f"tab_words{a}", align_bytes=64) for a in range(PASSES)]
         w_raw = [keep.tile([P, 4, M], F32, name=f"w_raw{a}", align_bytes=64) for a in range(PASSES)]
+        wgo_sb = keep.tile([P, S], F32, name="wgo_sb")
+        bias = [keep.tile([P, 1], F32, name=f"bias{h}") for h in range(HALVES)]
 
         def load_tab(a):
             nc.sync.dma_start(tab_words[a][:], tab[a, 0 : 512 * T].rearrange("(p x) -> p x", p=P).bitcast(I32))
@@ -51,10 +52,13 @@ def tile_list_tabscat_bias_kernel(tc, tab, w, b, wgo, offs, offs2, out):
                 tab[:, 512 * T + 4 * T * q : 512 * T + 4 * T * (q + 1)].rearrange("a (r t) -> a r t", r=4).bitcast(I32),
             )
 
+        def load_bias(queue, h):
+            queue.dma_start(bias[h][:], b[P * h : P * (h + 1)].unsqueeze(1))
+
+        nc.sync.dma_start(offs_sb[:], offs)
         load_tab(0)
-        bias = [keep.tile([P, 1], F32, name=f"bias{h}") for h in range(HALVES)]
         for h in range(HALVES):
-            nc.gpsimd.dma_start(bias[h][:], b[128 * h : 128 * (h + 1)].unsqueeze(1))
+            load_bias(nc.gpsimd, h)
         load_scales(nc.scalar, 0)
         load_scales(nc.scalar, 1)
         load_w(0)
@@ -65,7 +69,6 @@ def tile_list_tabscat_bias_kernel(tc, tab, w, b, wgo, offs, offs2, out):
         load_w(2)
         load_tab(2)
         nc.sync.dma_start(offs2_sb[:], offs2)
-        wgo_sb = keep.tile([P, S], F32, name="wgo_sb")
         nc.sync.dma_start(wgo_sb[:], wgo)
 
         warm = keep.tile([P, 1], F32, name="warm")
@@ -78,65 +81,74 @@ def tile_list_tabscat_bias_kernel(tc, tab, w, b, wgo, offs, offs2, out):
 
         words = [keep.tile([P, S], U32, name=f"words{a}", align_bytes=64) for a in range(PASSES)]
         scales = keep.tile([P, S], U8, name="scales", align_bytes=64)
-        w_bf = [keep.tile([P, M, 4], BF16, name=f"w_bf{a}", align_bytes=64) for a in range(2)]
-        w_bf_last = [keep.tile([P, 128, 4], BF16, name=f"w_bf_last{h}", align_bytes=64) for h in range(HALVES)]
+        w_bf = [keep.tile([P, M, 4], BF16, name=f"w_bf{a}", align_bytes=64) for a in range(PASSES)]
         w_words = [keep.tile([P, M], U32, name=f"w_words{a}", align_bytes=64) for a in range(PASSES)]
         w_scales = [keep.tile([P, M], U8, name=f"w_scales{a}", align_bytes=64) for a in range(PASSES)]
-        acc0 = [psum.tile([P, PIECE], F32, name=f"acc0{c}") for c in range(PIECES)]
-        acc1 = psum.tile([P, S], F32, name="acc1")
-        y0 = [keep.tile([P, PIECE], F32, name=f"y0{c}") for c in range(PIECES)]
-        y1 = keep.tile([P, S], F32, name="y1")
+        acc = [[psum.tile([P, CUTS[c + 1] - CUTS[c]], F32, name=f"acc{h}{c}") for c in range(PIECES)] for h in range(HALVES)]
+        y = [[keep.tile([P, CUTS[c + 1] - CUTS[c]], F32, name=f"y{h}{c}") for c in range(PIECES)] for h in range(HALVES)]
 
         def gather_words(a, first=0, end=S):
             nc.vector.tensor_copy(words[a][:, first:end], tab_words[a][:].bitcast(U32).indirect(offs_sb[:, first // 16 : end // 16]))
 
-        def quantise_w(a, cols, rounded):
-            nc.scalar.copy(
-                rounded.rearrange("p (c i) j -> p c j i", i=4),
-                w_raw[a][:, :, cols].rearrange("p j (c i) -> p c j i", i=4),
-            )
-            nc.vector.quantize_mx(w_words[a][:, cols].bitcast(FP8X4), w_scales[a][:, cols], rounded.rearrange("p n j -> p (n j)"))
+        def gather_scales():
+            nc.vector.tensor_copy(scales[:], scale_tab[:].bitcast(U8).indirect(offs_sb[:]))
 
-        def multiply(acc, a, h, cols):
-            rows = slice(128 * h, 128 * (h + 1))
-            nc.tensor.matmul_mx(
-                acc[:],
-                lhsT=w_words[a][:, rows].bitcast(FP8X4),
-                lhsT_scale=w_scales[a][:, rows],
-                rhs=words[a][:, cols].bitcast(FP8X4),
-                rhs_scale=scales[4 * a : P, cols],
-                start=(a == 0),
-                stop=(a == PASSES - 1),
+        def round_w(copy, a, first=0, end=M):
+            copy(
+                w_bf[a][:, first:end].rearrange("p (c i) j -> p c j i", i=4),
+                w_raw[a][:, :, first:end].rearrange("p j (c i) -> p c j i", i=4),
             )
 
-        def scatter(h, values, first, count):
+        def quantise_w(a, first=0, end=M):
+            nc.vector.quantize_mx(
+                w_words[a][:, first:end].bitcast(FP8X4), w_scales[a][:, first:end], w_bf[a][:, first:end].rearrange("p n j -> p (n j)")
+            )
+
+        def multiply(h, c, a):
+            rows = slice(P * h, P * (h + 1))
+            spans = [(CUTS[c], CUTS[c + 1])] if CUTS[c + 1] - CUTS[c] != 384 else [(CUTS[c], CUTS[c] + 128), (CUTS[c] + 128, CUTS[c + 1])]
+            for first, end in spans:
+                nc.tensor.matmul_mx(
+                    acc[h][c][:, first - CUTS[c] : end - CUTS[c]],
+                    lhsT=w_words[a][:, rows].bitcast(FP8X4),
+                    lhsT_scale=w_scales[a][:, rows],
+                    rhs=words[a][:, first:end].bitcast(FP8X4),
+                    rhs_scale=scales[4 * a : P, first:end],
+                    start=(a == 0 and first == CUTS[c]),
+                    stop=(a == PASSES - 1 and end == CUTS[c + 1]),
+                )
+
+        def empty(h, c):
+            nc.scalar.activation(y[h][c][:], acc[h][c][:], IDENT, bias=bias[h][:])
+
+        def scatter(h, c):
             nc.vector.tensor_tensor(
-                placed[h][:].indirect(offs2_sb[:, first // 16 : (first + count) // 16]),
-                values,
-                wgo_sb[:, first : first + count],
+                placed[h][:].indirect(offs2_sb[:, CUTS[c] // 16 : CUTS[c + 1] // 16]),
+                y[h][c][:],
+                wgo_sb[:, CUTS[c] : CUTS[c + 1]],
                 MULT,
             )
 
-        pieces = [slice(PIECE * c, PIECE * (c + 1)) for c in range(PIECES)]
         gather_words(0)
-        nc.vector.tensor_copy(scales[:], scale_tab[:].bitcast(U8).indirect(offs_sb[:]))
-        gather_words(1)
-        for a in range(2):
-            quantise_w(a, slice(0, M), w_bf[a][:])
-        for h in range(HALVES):
-            quantise_w(2, slice(128 * h, 128 * (h + 1)), w_bf_last[h][:])
-        for a in range(2):
+        gather_scales()
+        for a in range(PASSES - 1):
+            round_w(nc.scalar.copy, a)
+            quantise_w(a)
+            if a == 0:
+                gather_words(1)
             for c in range(PIECES):
-                multiply(acc0[c], a, 0, pieces[c])
+                for h in range(HALVES):
+                    multiply(h, c, a)
+        round_w(nc.scalar.copy, 2, 0, P)
+        round_w(nc.vector.tensor_copy, 2, P, M)
+        quantise_w(2)
         for c in range(PIECES):
-            gather_words(2, PIECE * c, PIECE * (c + 1))
-            multiply(acc0[c], 2, 0, pieces[c])
-            nc.scalar.activation(y0[c][:], acc0[c][:], IDENT, bias=bias[0][:])
-        for a in range(PASSES):
-            multiply(acc1, a, 1, slice(0, S))
-        nc.scalar.activation(y1[:], acc1[:], IDENT, bias=bias[1][:])
+            gather_words(2, CUTS[c], CUTS[c + 1])
+            for h in range(HALVES):
+                multiply(h, c, 2)
         for c in range(PIECES):
-            scatter(0, y0[c][:], PIECE * c, PIECE)
-        nc.sync.dma_start(out[0:P, :], placed[0][:])
-        scatter(1, y1[:], 0, S)
-        nc.sync.dma_start(out[P : 2 * P, :], placed[1][:])
+            for h in range(HALVES):
+                empty(h, c)
+                scatter(h, c)
+        for h in range(HALVES):
+            nc.sync.dma_start(out[P * h : P * (h + 1), :], placed[h][:])

@@ -16,10 +16,18 @@ MULT = mybir.AluOpType.mult
 IDENT = mybir.ActivationFunctionType.Identity
 
 P = 128
-PASSES = K // 512
-HALVES = M // 128
-CUTS = [0, 128, S]
-PIECES = len(CUTS) - 1
+PACK = 4
+K_PASS = P * PACK
+PASSES = K // K_PASS
+LAST = PASSES - 1
+HALVES = M // P
+PER_COLUMN = 16
+QUADRANT = 32
+SCALE_ROWS = 4
+
+FIRST_PIECE = 128
+PIECES = [(0, FIRST_PIECE), (FIRST_PIECE, S)]
+SPANS = [[(0, 128)], [(128, 256), (256, S)]]
 
 
 def tile_list_tabscat_bias_kernel(tc, tab, w, b, wgo, offs, offs2, out):
@@ -29,36 +37,34 @@ def tile_list_tabscat_bias_kernel(tc, tab, w, b, wgo, offs, offs2, out):
         keep = ctx.enter_context(tc.tile_pool(name="keep", bufs=1))
         psum = ctx.enter_context(tc.psum_pool(name="psum", bufs=1))
 
-        offs_sb = lists.tile([P, S // 16], U16, name="offs_sb")
-        offs2_sb = lists.tile([P, S // 16], U16, name="offs2_sb")
+        offs_sb = lists.tile([P, S // PER_COLUMN], U16, name="offs_sb")
+        offs2_sb = lists.tile([P, S // PER_COLUMN], U16, name="offs2_sb")
 
-        scale_tab = keep.tile([P, T // 4], I32, name="scale_tab", align_bytes=64)
-        nc.gpsimd.memset(scale_tab[:], 0)
+        tab_scales = keep.tile([P, T // 4], I32, name="tab_scales", align_bytes=64)
+        nc.gpsimd.memset(tab_scales[:], 0)
 
         tab_words = [keep.tile([P, T], I32, name=f"tab_words{a}", align_bytes=64) for a in range(PASSES)]
-        w_raw = [keep.tile([P, 4, M], F32, name=f"w_raw{a}", align_bytes=64) for a in range(PASSES)]
+        w_raw = [keep.tile([P, PACK, M], F32, name=f"w_raw{a}", align_bytes=64) for a in range(PASSES)]
         wgo_sb = keep.tile([P, S], F32, name="wgo_sb")
         bias = [keep.tile([P, 1], F32, name=f"bias{h}") for h in range(HALVES)]
 
         def load_tab(a):
-            nc.sync.dma_start(tab_words[a][:], tab[a, 0 : 512 * T].rearrange("(p x) -> p x", p=P).bitcast(I32))
+            nc.sync.dma_start(tab_words[a][:], tab[a, 0 : K_PASS * T].rearrange("(p x) -> p x", p=P).bitcast(I32))
 
         def load_w(a):
-            nc.sync.dma_start(w_raw[a][:], w[512 * a : 512 * (a + 1), :].rearrange("(p j) n -> p j n", j=4))
+            nc.sync.dma_start(w_raw[a][:], w[K_PASS * a : K_PASS * (a + 1), :].rearrange("(p j) n -> p j n", j=PACK))
 
         def load_scales(queue, q):
+            first = (K_PASS + SCALE_ROWS * q) * T
             queue.dma_start(
-                scale_tab[32 * q : 32 * q + 12, :],
-                tab[:, 512 * T + 4 * T * q : 512 * T + 4 * T * (q + 1)].rearrange("a (r t) -> a r t", r=4).bitcast(I32),
+                tab_scales[QUADRANT * q : QUADRANT * q + SCALE_ROWS * PASSES, :],
+                tab[:, first : first + SCALE_ROWS * T].rearrange("a (r t) -> a r t", r=SCALE_ROWS).bitcast(I32),
             )
 
-        def load_bias(queue, h):
-            queue.dma_start(bias[h][:], b[P * h : P * (h + 1)].unsqueeze(1))
-
-        nc.sync.dma_start(offs_sb[:], offs)
         load_tab(0)
+        nc.sync.dma_start(offs_sb[:], offs)
         for h in range(HALVES):
-            load_bias(nc.gpsimd, h)
+            nc.gpsimd.dma_start(bias[h][:], b[P * h : P * (h + 1)].unsqueeze(1))
         load_scales(nc.scalar, 0)
         load_scales(nc.scalar, 1)
         load_w(0)
@@ -66,89 +72,84 @@ def tile_list_tabscat_bias_kernel(tc, tab, w, b, wgo, offs, offs2, out):
         load_scales(nc.sync, 3)
         load_tab(1)
         load_w(1)
-        load_w(2)
-        load_tab(2)
+        load_w(LAST)
+        load_tab(LAST)
         nc.sync.dma_start(offs2_sb[:], offs2)
         nc.sync.dma_start(wgo_sb[:], wgo)
-
-        warm = keep.tile([P, 1], F32, name="warm")
-        nc.vector.memset(warm[:], 0.0)
-        nc.scalar.activation(warm[:], warm[:], IDENT)
 
         placed = [keep.tile([P, T], F32, name=f"placed{h}") for h in range(HALVES)]
         for h in range(HALVES):
             nc.vector.memset(placed[h][:], 0.0)
 
-        words = [keep.tile([P, S], U32, name=f"words{a}", align_bytes=64) for a in range(PASSES)]
+        words = {}
         scales = keep.tile([P, S], U8, name="scales", align_bytes=64)
-        w_bf = [keep.tile([P, M, 4], BF16, name=f"w_bf{a}", align_bytes=64) for a in range(PASSES)]
+        w_bf = [keep.tile([P, M, PACK], BF16, name=f"w_bf{a}", tag=f"w_bf{a}", align_bytes=64) for a in range(PASSES)]
         w_words = [keep.tile([P, M], U32, name=f"w_words{a}", align_bytes=64) for a in range(PASSES)]
         w_scales = [keep.tile([P, M], U8, name=f"w_scales{a}", align_bytes=64) for a in range(PASSES)]
-        acc = [[psum.tile([P, CUTS[c + 1] - CUTS[c]], F32, name=f"acc{h}{c}") for c in range(PIECES)] for h in range(HALVES)]
-        y = [[keep.tile([P, CUTS[c + 1] - CUTS[c]], F32, name=f"y{h}{c}") for c in range(PIECES)] for h in range(HALVES)]
+        acc = [[psum.tile([P, end - first], F32, name=f"acc{h}{c}") for c, (first, end) in enumerate(PIECES)] for h in range(HALVES)]
+        y = [[keep.tile([P, end - first], F32, name=f"y{h}{c}") for c, (first, end) in enumerate(PIECES)] for h in range(HALVES)]
 
-        def gather_words(a, first=0, end=S):
-            nc.vector.tensor_copy(words[a][:, first:end], tab_words[a][:].bitcast(U32).indirect(offs_sb[:, first // 16 : end // 16]))
+        def entries(list_tile, first, end):
+            return list_tile[:, first // PER_COLUMN : end // PER_COLUMN]
 
-        def gather_scales():
-            nc.vector.tensor_copy(scales[:], scale_tab[:].bitcast(U8).indirect(offs_sb[:]))
+        def new_words(a, tag):
+            words[a] = keep.tile([P, S], U32, name=f"words{a}", tag=tag, align_bytes=64)
 
-        def round_w(copy, a, first=0, end=M):
+        def gather_words(a, first, end):
+            nc.vector.tensor_copy(words[a][:, first:end], tab_words[a][:].bitcast(U32).indirect(entries(offs_sb, first, end)))
+
+        def round_w(copy, a, first, end):
             copy(
                 w_bf[a][:, first:end].rearrange("p (c i) j -> p c j i", i=4),
                 w_raw[a][:, :, first:end].rearrange("p j (c i) -> p c j i", i=4),
             )
 
-        def quantise_w(a, first=0, end=M):
-            nc.vector.quantize_mx(
-                w_words[a][:, first:end].bitcast(FP8X4), w_scales[a][:, first:end], w_bf[a][:, first:end].rearrange("p n j -> p (n j)")
-            )
+        def quantise_w(a):
+            nc.vector.quantize_mx(w_words[a][:].bitcast(FP8X4), w_scales[a][:], w_bf[a][:].rearrange("p n j -> p (n j)"))
 
         def multiply(h, c, a):
-            rows = slice(P * h, P * (h + 1))
-            spans = [(CUTS[c], CUTS[c + 1])] if CUTS[c + 1] - CUTS[c] != 384 else [(CUTS[c], CUTS[c] + 128), (CUTS[c] + 128, CUTS[c + 1])]
-            for first, end in spans:
+            channels = slice(P * h, P * (h + 1))
+            piece_first, piece_end = PIECES[c]
+            for first, end in SPANS[c]:
                 nc.tensor.matmul_mx(
-                    acc[h][c][:, first - CUTS[c] : end - CUTS[c]],
-                    lhsT=w_words[a][:, rows].bitcast(FP8X4),
-                    lhsT_scale=w_scales[a][:, rows],
+                    acc[h][c][:, first - piece_first : end - piece_first],
+                    lhsT=w_words[a][:, channels].bitcast(FP8X4),
+                    lhsT_scale=w_scales[a][:, channels],
                     rhs=words[a][:, first:end].bitcast(FP8X4),
-                    rhs_scale=scales[4 * a : P, first:end],
-                    start=(a == 0 and first == CUTS[c]),
-                    stop=(a == PASSES - 1 and end == CUTS[c + 1]),
+                    rhs_scale=scales[SCALE_ROWS * a : P, first:end],
+                    start=(a == 0 and first == piece_first),
+                    stop=(a == LAST and end == piece_end),
                 )
 
-        def empty(h, c):
-            nc.scalar.activation(y[h][c][:], acc[h][c][:], IDENT, bias=bias[h][:])
-
-        def scatter(h, c):
-            nc.vector.tensor_tensor(
-                placed[h][:].indirect(offs2_sb[:, CUTS[c] // 16 : CUTS[c + 1] // 16]),
-                y[h][c][:],
-                wgo_sb[:, CUTS[c] : CUTS[c + 1]],
-                MULT,
-            )
-
-        gather_words(0)
-        gather_scales()
-        for a in range(PASSES - 1):
-            round_w(nc.scalar.copy, a)
-            quantise_w(a)
-            if a == 0:
-                gather_words(1)
-            for c in range(PIECES):
+        def multiply_pass(a):
+            for c in range(len(PIECES)):
                 for h in range(HALVES):
                     multiply(h, c, a)
-        round_w(nc.scalar.copy, 2, 0, P)
-        round_w(nc.vector.tensor_copy, 2, P, M)
-        quantise_w(2)
-        for c in range(PIECES):
-            gather_words(2, CUTS[c], CUTS[c + 1])
+
+        new_words(0, "words0")
+        gather_words(0, 0, S)
+        nc.vector.tensor_copy(scales[:], tab_scales[:].bitcast(U8).indirect(offs_sb[:]))
+        round_w(nc.scalar.copy, 0, 0, M)
+        quantise_w(0)
+        new_words(1, "w_bf0")
+        gather_words(1, 0, S)
+        multiply_pass(0)
+        round_w(nc.scalar.copy, 1, 0, M)
+        quantise_w(1)
+        multiply_pass(1)
+
+        round_w(nc.scalar.copy, LAST, 0, P)
+        round_w(nc.vector.tensor_copy, LAST, P, M)
+        quantise_w(LAST)
+        new_words(LAST, "words2")
+        for c, (first, end) in enumerate(PIECES):
+            gather_words(LAST, first, end)
             for h in range(HALVES):
-                multiply(h, c, 2)
-        for c in range(PIECES):
+                multiply(h, c, LAST)
+
+        for c, (first, end) in enumerate(PIECES):
             for h in range(HALVES):
-                empty(h, c)
-                scatter(h, c)
+                nc.scalar.activation(y[h][c][:], acc[h][c][:], IDENT, bias=bias[h][:])
+                nc.vector.tensor_tensor(placed[h][:].indirect(entries(offs2_sb, first, end)), y[h][c][:], wgo_sb[:, first:end], MULT)
         for h in range(HALVES):
             nc.sync.dma_start(out[P * h : P * (h + 1), :], placed[h][:])

@@ -46,7 +46,7 @@ def tile_list_tabscat_bias_kernel(tc, tab, w, b, wgo, offs, offs2, out):
         tab_words = [keep.tile([P, T], I32, name=f"tab_words{a}", align_bytes=64) for a in range(PASSES)]
         w_raw = [keep.tile([P, PACK, M], F32, name=f"w_raw{a}", align_bytes=64) for a in range(PASSES)]
         wgo_sb = keep.tile([P, S], F32, name="wgo_sb")
-        bias = [keep.tile([P, 1], F32, name=f"bias{h}") for h in range(HALVES)]
+        bias = keep.tile([P, HALVES], F32, name="bias")
 
         def load_tab(a):
             nc.sync.dma_start(tab_words[a][:], tab[a, 0 : K_PASS * T].rearrange("(p x) -> p x", p=P).bitcast(I32))
@@ -63,8 +63,7 @@ def tile_list_tabscat_bias_kernel(tc, tab, w, b, wgo, offs, offs2, out):
 
         load_tab(0)
         nc.sync.dma_start(offs_sb[:], offs)
-        for h in range(HALVES):
-            nc.gpsimd.dma_start(bias[h][:], b[P * h : P * (h + 1)].unsqueeze(1))
+        nc.gpsimd.dma_start(bias[:], b.rearrange("(p h) -> p h", h=HALVES))
         load_scales(nc.scalar, 0)
         load_scales(nc.scalar, 1)
         load_w(0)
@@ -77,31 +76,32 @@ def tile_list_tabscat_bias_kernel(tc, tab, w, b, wgo, offs, offs2, out):
         nc.sync.dma_start(offs2_sb[:], offs2)
         nc.sync.dma_start(wgo_sb[:], wgo)
 
+        warm = keep.tile([P, 1], F32, name="warm")
+        nc.vector.memset(warm[:], 0.0)
+        nc.scalar.activation(warm[:], warm[:], IDENT)
+
         placed = [keep.tile([P, T], F32, name=f"placed{h}") for h in range(HALVES)]
         for h in range(HALVES):
             nc.vector.memset(placed[h][:], 0.0)
 
-        words = {}
+        words = [keep.tile([P, S], U32, name=f"words{a}", align_bytes=64) for a in range(PASSES)]
         scales = keep.tile([P, S], U8, name="scales", align_bytes=64)
-        w_bf = [keep.tile([P, M, PACK], BF16, name=f"w_bf{a}", tag=f"w_bf{a}", align_bytes=64) for a in range(PASSES)]
+        w_bf = [keep.tile([P, M, PACK], BF16, name=f"w_bf{a}", align_bytes=64) for a in range(PASSES)]
         w_words = [keep.tile([P, M], U32, name=f"w_words{a}", align_bytes=64) for a in range(PASSES)]
         w_scales = [keep.tile([P, M], U8, name=f"w_scales{a}", align_bytes=64) for a in range(PASSES)]
-        acc = [[psum.tile([P, end - first], F32, name=f"acc{h}{c}") for c, (first, end) in enumerate(PIECES)] for h in range(HALVES)]
+        acc = [{first: psum.tile([P, end - first], F32, name=f"acc{h}_{first}") for spans in SPANS for first, end in spans} for h in range(HALVES)]
         y = [[keep.tile([P, end - first], F32, name=f"y{h}{c}") for c, (first, end) in enumerate(PIECES)] for h in range(HALVES)]
 
         def entries(list_tile, first, end):
             return list_tile[:, first // PER_COLUMN : end // PER_COLUMN]
-
-        def new_words(a, tag):
-            words[a] = keep.tile([P, S], U32, name=f"words{a}", tag=tag, align_bytes=64)
 
         def gather_words(a, first, end):
             nc.vector.tensor_copy(words[a][:, first:end], tab_words[a][:].bitcast(U32).indirect(entries(offs_sb, first, end)))
 
         def round_w(copy, a, first, end):
             copy(
-                w_bf[a][:, first:end].rearrange("p (c i) j -> p c j i", i=4),
-                w_raw[a][:, :, first:end].rearrange("p j (c i) -> p c j i", i=4),
+                w_bf[a][:].rearrange("p (h c i) j -> p c j i h", h=HALVES, i=2)[:, first // 4 : end // 4],
+                w_raw[a][:, :, first:end].rearrange("p j (c i h) -> p c j i h", h=HALVES, i=2),
             )
 
         def quantise_w(a):
@@ -109,16 +109,15 @@ def tile_list_tabscat_bias_kernel(tc, tab, w, b, wgo, offs, offs2, out):
 
         def multiply(h, c, a):
             channels = slice(P * h, P * (h + 1))
-            piece_first, piece_end = PIECES[c]
             for first, end in SPANS[c]:
                 nc.tensor.matmul_mx(
-                    acc[h][c][:, first - piece_first : end - piece_first],
+                    acc[h][first][:],
                     lhsT=w_words[a][:, channels].bitcast(FP8X4),
                     lhsT_scale=w_scales[a][:, channels],
                     rhs=words[a][:, first:end].bitcast(FP8X4),
                     rhs_scale=scales[SCALE_ROWS * a : P, first:end],
-                    start=(a == 0 and first == piece_first),
-                    stop=(a == LAST and end == piece_end),
+                    start=(a == 0),
+                    stop=(a == LAST),
                 )
 
         def multiply_pass(a):
@@ -126,12 +125,10 @@ def tile_list_tabscat_bias_kernel(tc, tab, w, b, wgo, offs, offs2, out):
                 for h in range(HALVES):
                     multiply(h, c, a)
 
-        new_words(0, "words0")
         gather_words(0, 0, S)
         nc.vector.tensor_copy(scales[:], tab_scales[:].bitcast(U8).indirect(offs_sb[:]))
         round_w(nc.scalar.copy, 0, 0, M)
         quantise_w(0)
-        new_words(1, "w_bf0")
         gather_words(1, 0, S)
         multiply_pass(0)
         round_w(nc.scalar.copy, 1, 0, M)
@@ -141,7 +138,6 @@ def tile_list_tabscat_bias_kernel(tc, tab, w, b, wgo, offs, offs2, out):
         round_w(nc.scalar.copy, LAST, 0, P)
         round_w(nc.vector.tensor_copy, LAST, P, M)
         quantise_w(LAST)
-        new_words(LAST, "words2")
         for c, (first, end) in enumerate(PIECES):
             gather_words(LAST, first, end)
             for h in range(HALVES):
@@ -149,7 +145,8 @@ def tile_list_tabscat_bias_kernel(tc, tab, w, b, wgo, offs, offs2, out):
 
         for c, (first, end) in enumerate(PIECES):
             for h in range(HALVES):
-                nc.scalar.activation(y[h][c][:], acc[h][c][:], IDENT, bias=bias[h][:])
+                for span_first, span_end in SPANS[c]:
+                    nc.scalar.activation(y[h][c][:, span_first - first : span_end - first], acc[h][span_first][:], IDENT, bias=bias[:, h : h + 1])
                 nc.vector.tensor_tensor(placed[h][:].indirect(entries(offs2_sb, first, end)), y[h][c][:], wgo_sb[:, first:end], MULT)
         for h in range(HALVES):
-            nc.sync.dma_start(out[P * h : P * (h + 1), :], placed[h][:])
+            nc.sync.dma_start(out.rearrange("(p h) t -> h p t", h=HALVES)[h], placed[h][:])

@@ -63,7 +63,6 @@ def tile_list_tabscat_bias_kernel(tc, tab, w, b, wgo, offs, offs2, out):
 
         load_tab(0)
         nc.sync.dma_start(offs_sb[:], offs)
-        nc.gpsimd.dma_start(bias[:], b.rearrange("(p h) -> p h", h=HALVES))
         load_scales(nc.scalar, 0)
         load_scales(nc.scalar, 1)
         load_w(0)
@@ -73,6 +72,7 @@ def tile_list_tabscat_bias_kernel(tc, tab, w, b, wgo, offs, offs2, out):
         load_w(1)
         load_w(LAST)
         load_tab(LAST)
+        nc.sync.dma_start(bias[:], b.rearrange("(p h) -> p h", h=HALVES))
         nc.sync.dma_start(offs2_sb[:], offs2)
         nc.sync.dma_start(wgo_sb[:], wgo)
 

@@ -76,17 +76,13 @@ def tile_list_tabscat_bias_kernel(tc, tab, w, b, wgo, offs, offs2, out):
         nc.sync.dma_start(offs2_sb[:], offs2)
         nc.sync.dma_start(wgo_sb[:], wgo)
 
-        warm = keep.tile([P, 1], F32, name="warm")
-        nc.vector.memset(warm[:], 0.0)
-        nc.scalar.activation(warm[:], warm[:], IDENT)
-
         placed = [keep.tile([P, T], F32, name=f"placed{h}") for h in range(HALVES)]
         for h in range(HALVES):
             nc.vector.memset(placed[h][:], 0.0)
 
-        words = [keep.tile([P, S], U32, name=f"words{a}", align_bytes=64) for a in range(PASSES)]
+        words = {}
         scales = keep.tile([P, S], U8, name="scales", align_bytes=64)
-        w_bf = [keep.tile([P, M, PACK], BF16, name=f"w_bf{a}", align_bytes=64) for a in range(PASSES)]
+        w_bf = [keep.tile([P, M, PACK], BF16, name=f"w_bf{a}", tag=f"w_bf{a}", align_bytes=64) for a in range(PASSES)]
         w_words = [keep.tile([P, M], U32, name=f"w_words{a}", align_bytes=64) for a in range(PASSES)]
         w_scales = [keep.tile([P, M], U8, name=f"w_scales{a}", align_bytes=64) for a in range(PASSES)]
         acc = [{first: psum.tile([P, end - first], F32, name=f"acc{h}_{first}") for spans in SPANS for first, end in spans} for h in range(HALVES)]
@@ -94,6 +90,9 @@ def tile_list_tabscat_bias_kernel(tc, tab, w, b, wgo, offs, offs2, out):
 
         def entries(list_tile, first, end):
             return list_tile[:, first // PER_COLUMN : end // PER_COLUMN]
+
+        def new_words(a, tag):
+            words[a] = keep.tile([P, S], U32, name=f"words{a}", tag=tag, align_bytes=64)
 
         def gather_words(a, first, end):
             nc.vector.tensor_copy(words[a][:, first:end], tab_words[a][:].bitcast(U32).indirect(entries(offs_sb, first, end)))
@@ -125,10 +124,12 @@ def tile_list_tabscat_bias_kernel(tc, tab, w, b, wgo, offs, offs2, out):
                 for h in range(HALVES):
                     multiply(h, c, a)
 
+        new_words(0, "words0")
         gather_words(0, 0, S)
         nc.vector.tensor_copy(scales[:], tab_scales[:].bitcast(U8).indirect(offs_sb[:]))
         round_w(nc.scalar.copy, 0, 0, M)
         quantise_w(0)
+        new_words(1, "w_bf0")
         gather_words(1, 0, S)
         multiply_pass(0)
         round_w(nc.scalar.copy, 1, 0, M)
@@ -138,6 +139,7 @@ def tile_list_tabscat_bias_kernel(tc, tab, w, b, wgo, offs, offs2, out):
         round_w(nc.scalar.copy, LAST, 0, P)
         round_w(nc.vector.tensor_copy, LAST, P, M)
         quantise_w(LAST)
+        new_words(LAST, "words2")
         for c, (first, end) in enumerate(PIECES):
             gather_words(LAST, first, end)
             for h in range(HALVES):

@@ -103,6 +103,20 @@ def tile_list_tabscat_bias_kernel(tc, tab, w, b, wgo, offs, offs2, out):
                 w_raw[a][:, :, first:end].rearrange("p j (c i h) -> p c j i h", h=HALVES, i=2),
             )
 
+        def round_half(copy, a, h):
+            copy(
+                w_bf[a][:, P * h : P * (h + 1), :].rearrange("p (c i) j -> p c j i", i=PACK),
+                w_raw[a][:].rearrange("p j (c i h) -> p h c j i", h=HALVES, i=PACK)[:, h],
+            )
+
+        def quantise_half(a, h):
+            channels = slice(P * h, P * (h + 1))
+            nc.vector.quantize_mx(
+                w_words[a][:, channels].bitcast(FP8X4),
+                w_scales[a][:, channels],
+                w_bf[a][:, channels, :].rearrange("p n j -> p (n j)"),
+            )
+
         def quantise_w(a):
             nc.vector.quantize_mx(w_words[a][:].bitcast(FP8X4), w_scales[a][:], w_bf[a][:].rearrange("p n j -> p (n j)"))
 
@@ -136,12 +150,14 @@ def tile_list_tabscat_bias_kernel(tc, tab, w, b, wgo, offs, offs2, out):
         quantise_w(1)
         multiply_pass(1)
 
-        round_w(nc.scalar.copy, LAST, 0, P)
-        round_w(nc.vector.tensor_copy, LAST, P, M)
-        quantise_w(LAST)
+        for h in range(HALVES):
+            round_half(nc.scalar.copy, LAST, h)
+        quantise_half(LAST, 0)
         new_words(LAST, "words2")
         for c, (first, end) in enumerate(PIECES):
             gather_words(LAST, first, end)
+            if c == 0:
+                quantise_half(LAST, 1)
             for h in range(HALVES):
                 multiply(h, c, LAST)
 

@@ -41,7 +41,7 @@ def tile_list_tabscat_bias_kernel(tc, tab, w, b, wgo, offs, offs2, out):
         offs2_sb = lists.tile([P, S // PER_COLUMN], U16, name="offs2_sb")
 
         tab_scales = keep.tile([P, T // 4], I32, name="tab_scales", align_bytes=64)
-        nc.gpsimd.memset(tab_scales[:], 0)
+        nc.vector.memset(tab_scales[:], 0)
 
         tab_words = [keep.tile([P, T], I32, name=f"tab_words{a}", align_bytes=64) for a in range(PASSES)]
         w_raw = [keep.tile([P, PACK, M], F32, name=f"w_raw{a}", align_bytes=64) for a in range(PASSES)]

@@ -24,10 +24,12 @@ HALVES = M // P
 PER_COLUMN = 16
 QUADRANT = 32
 SCALE_ROWS = 4
+WORD_BYTES = 4
+RUN = 4
 
 FIRST_PIECE = 128
 PIECES = [(0, FIRST_PIECE), (FIRST_PIECE, S)]
-SPANS = [[(0, 128)], [(128, 256), (256, S)]]
+SPANS = [[(0, FIRST_PIECE)], [(FIRST_PIECE, 2 * FIRST_PIECE), (2 * FIRST_PIECE, S)]]
 
 
 def tile_list_tabscat_bias_kernel(tc, tab, w, b, wgo, offs, offs2, out):
@@ -40,7 +42,7 @@ def tile_list_tabscat_bias_kernel(tc, tab, w, b, wgo, offs, offs2, out):
         offs_sb = lists.tile([P, S // PER_COLUMN], U16, name="offs_sb")
         offs2_sb = lists.tile([P, S // PER_COLUMN], U16, name="offs2_sb")
 
-        tab_scales = keep.tile([P, T // 4], I32, name="tab_scales", align_bytes=64)
+        tab_scales = keep.tile([P, T // WORD_BYTES], I32, name="tab_scales", align_bytes=64)
         nc.vector.memset(tab_scales[:], 0)
 
         tab_words = [keep.tile([P, T], I32, name=f"tab_words{a}", align_bytes=64) for a in range(PASSES)]
@@ -85,8 +87,14 @@ def tile_list_tabscat_bias_kernel(tc, tab, w, b, wgo, offs, offs2, out):
         w_bf = [keep.tile([P, M, PACK], BF16, name=f"w_bf{a}", tag=f"w_bf{a}", align_bytes=64) for a in range(PASSES)]
         w_words = [keep.tile([P, M], U32, name=f"w_words{a}", align_bytes=64) for a in range(PASSES)]
         w_scales = [keep.tile([P, M], U8, name=f"w_scales{a}", align_bytes=64) for a in range(PASSES)]
-        acc = [{first: psum.tile([P, end - first], F32, name=f"acc{h}_{first}") for spans in SPANS for first, end in spans} for h in range(HALVES)]
-        y = [[keep.tile([P, end - first], F32, name=f"y{h}{c}") for c, (first, end) in enumerate(PIECES)] for h in range(HALVES)]
+        acc = [
+            {first: psum.tile([P, end - first], F32, name=f"acc{h}_{first}") for spans in SPANS for first, end in spans}
+            for h in range(HALVES)
+        ]
+        y = [
+            [keep.tile([P, end - first], F32, name=f"y{h}{piece}") for piece, (first, end) in enumerate(PIECES)]
+            for h in range(HALVES)
+        ]
 
         def entries(list_tile, first, end):
             return list_tile[:, first // PER_COLUMN : end // PER_COLUMN]
@@ -97,32 +105,28 @@ def tile_list_tabscat_bias_kernel(tc, tab, w, b, wgo, offs, offs2, out):
         def gather_words(a, first, end):
             nc.vector.tensor_copy(words[a][:, first:end], tab_words[a][:].bitcast(U32).indirect(entries(offs_sb, first, end)))
 
-        def round_w(copy, a, first, end):
-            copy(
-                w_bf[a][:].rearrange("p (h c i) j -> p c j i h", h=HALVES, i=2)[:, first // 4 : end // 4],
-                w_raw[a][:, :, first:end].rearrange("p j (c i h) -> p c j i h", h=HALVES, i=2),
+        def round_w(a):
+            nc.scalar.copy(
+                w_bf[a][:].rearrange("p (h c i) j -> p c j i h", h=HALVES, i=RUN // HALVES),
+                w_raw[a][:].rearrange("p j (c i h) -> p c j i h", h=HALVES, i=RUN // HALVES),
             )
 
-        def round_half(copy, a, h):
-            copy(
-                w_bf[a][:, P * h : P * (h + 1), :].rearrange("p (c i) j -> p c j i", i=PACK),
-                w_raw[a][:].rearrange("p j (c i h) -> p h c j i", h=HALVES, i=PACK)[:, h],
+        def round_half(a, h):
+            nc.scalar.copy(
+                w_bf[a][:, P * h : P * (h + 1), :].rearrange("p (c i) j -> p c j i", i=RUN),
+                w_raw[a][:].rearrange("p j (c i h) -> p h c j i", h=HALVES, i=RUN)[:, h],
             )
 
-        def quantise_half(a, h):
-            channels = slice(P * h, P * (h + 1))
+        def quantise_w(a, first, end):
             nc.vector.quantize_mx(
-                w_words[a][:, channels].bitcast(FP8X4),
-                w_scales[a][:, channels],
-                w_bf[a][:, channels, :].rearrange("p n j -> p (n j)"),
+                w_words[a][:, first:end].bitcast(FP8X4),
+                w_scales[a][:, first:end],
+                w_bf[a][:, first:end, :].rearrange("p n j -> p (n j)"),
             )
 
-        def quantise_w(a):
-            nc.vector.quantize_mx(w_words[a][:].bitcast(FP8X4), w_scales[a][:], w_bf[a][:].rearrange("p n j -> p (n j)"))
-
-        def multiply(h, c, a):
+        def multiply(h, piece, a):
             channels = slice(P * h, P * (h + 1))
-            for first, end in SPANS[c]:
+            for first, end in SPANS[piece]:
                 nc.tensor.matmul_mx(
                     acc[h][first][:],
                     lhsT=w_words[a][:, channels].bitcast(FP8X4),
@@ -134,37 +138,46 @@ def tile_list_tabscat_bias_kernel(tc, tab, w, b, wgo, offs, offs2, out):
                 )
 
         def multiply_pass(a):
-            for c in range(len(PIECES)):
+            for piece in range(len(PIECES)):
                 for h in range(HALVES):
-                    multiply(h, c, a)
+                    multiply(h, piece, a)
 
         new_words(0, "words0")
         gather_words(0, 0, S)
         nc.vector.tensor_copy(scales[:], tab_scales[:].bitcast(U8).indirect(offs_sb[:]))
-        round_w(nc.scalar.copy, 0, 0, M)
-        quantise_w(0)
+        round_w(0)
+        quantise_w(0, 0, M)
         new_words(1, "w_bf0")
         gather_words(1, 0, S)
         multiply_pass(0)
-        round_w(nc.scalar.copy, 1, 0, M)
-        quantise_w(1)
-        multiply_pass(1)
+        for h in range(HALVES):
+            round_half(1, h)
+            quantise_w(1, P * h, P * (h + 1))
+            for piece in range(len(PIECES)):
+                multiply(h, piece, 1)
 
         for h in range(HALVES):
-            round_half(nc.scalar.copy, LAST, h)
-        quantise_half(LAST, 0)
+            round_half(LAST, h)
+        quantise_w(LAST, 0, P)
         new_words(LAST, "words2")
-        for c, (first, end) in enumerate(PIECES):
+        for piece, (first, end) in enumerate(PIECES):
             gather_words(LAST, first, end)
-            if c == 0:
-                quantise_half(LAST, 1)
+            if piece == 0:
+                quantise_w(LAST, P, M)
             for h in range(HALVES):
-                multiply(h, c, LAST)
+                multiply(h, piece, LAST)
 
-        for c, (first, end) in enumerate(PIECES):
+        for piece, (first, end) in enumerate(PIECES):
             for h in range(HALVES):
-                for span_first, span_end in SPANS[c]:
-                    nc.scalar.activation(y[h][c][:, span_first - first : span_end - first], acc[h][span_first][:], IDENT, bias=bias[:, h : h + 1])
-                nc.vector.tensor_tensor(placed[h][:].indirect(entries(offs2_sb, first, end)), y[h][c][:], wgo_sb[:, first:end], MULT)
+                for span_first, span_end in SPANS[piece]:
+                    nc.scalar.activation(
+                        y[h][piece][:, span_first - first : span_end - first],
+                        acc[h][span_first][:],
+                        IDENT,
+                        bias=bias[:, h : h + 1],
+                    )
+                nc.vector.tensor_tensor(
+                    placed[h][:].indirect(entries(offs2_sb, first, end)), y[h][piece][:], wgo_sb[:, first:end], MULT
+                )
         for h in range(HALVES):
             nc.sync.dma_start(out.rearrange("(p h) t -> h p t", h=HALVES)[h], placed[h][:])

from contextlib import ExitStack

import concourse.mybir as mybir

K, M, T, S = 1536, 256, 1024, 512
FLOPS = 2 * K * M * S

F32 = mybir.dt.float32
BF16 = mybir.dt.bfloat16
I32 = mybir.dt.int32
U32 = mybir.dt.uint32
U16 = mybir.dt.uint16
U8 = mybir.dt.uint8
FP8X4 = mybir.dt.float8_e4m3fn_x4
MULT = mybir.AluOpType.mult
IDENT = mybir.ActivationFunctionType.Identity

P = 128
PACK = 4
K_PASS = P * PACK
PASSES = K // K_PASS
LAST = PASSES - 1
HALVES = M // P
PER_COLUMN = 16
QUADRANT = 32
SCALE_ROWS = 4
WORD_BYTES = 4
RUN = 4

FIRST_PIECE = 128
PIECES = [(0, FIRST_PIECE), (FIRST_PIECE, S)]
SPANS = [[(0, FIRST_PIECE)], [(FIRST_PIECE, 2 * FIRST_PIECE), (2 * FIRST_PIECE, S)]]


def tile_list_tabscat_bias_kernel(tc, tab, w, b, wgo, offs, offs2, out):
    nc = tc.nc
    with ExitStack() as ctx:
        lists = ctx.enter_context(tc.tile_pool(name="lists", bufs=1))
        keep = ctx.enter_context(tc.tile_pool(name="keep", bufs=1))
        psum = ctx.enter_context(tc.psum_pool(name="psum", bufs=1))

        offs_sb = lists.tile([P, S // PER_COLUMN], U16, name="offs_sb")
        offs2_sb = lists.tile([P, S // PER_COLUMN], U16, name="offs2_sb")

        tab_scales = keep.tile([P, T // WORD_BYTES], I32, name="tab_scales", align_bytes=64)
        nc.vector.memset(tab_scales[:], 0)

        tab_words = [keep.tile([P, T], I32, name=f"tab_words{a}", align_bytes=64) for a in range(PASSES)]
        w_raw = [keep.tile([P, PACK, M], F32, name=f"w_raw{a}", align_bytes=64) for a in range(PASSES)]
        wgo_sb = keep.tile([P, S], F32, name="wgo_sb")
        bias = keep.tile([P, HALVES], F32, name="bias")

        def load_tab(a):
            nc.sync.dma_start(tab_words[a][:], tab[a, 0 : K_PASS * T].rearrange("(p x) -> p x", p=P).bitcast(I32))

        def load_w(a):
            nc.sync.dma_start(w_raw[a][:], w[K_PASS * a : K_PASS * (a + 1), :].rearrange("(p j) n -> p j n", j=PACK))

        def load_scales(queue, q):
            first = (K_PASS + SCALE_ROWS * q) * T
            queue.dma_start(
                tab_scales[QUADRANT * q : QUADRANT * q + SCALE_ROWS * PASSES, :],
                tab[:, first : first + SCALE_ROWS * T].rearrange("a (r t) -> a r t", r=SCALE_ROWS).bitcast(I32),
            )

        load_tab(0)
        nc.sync.dma_start(offs_sb[:], offs)
        load_scales(nc.scalar, 0)
        load_scales(nc.scalar, 1)
        load_w(0)
        load_scales(nc.sync, 2)
        load_scales(nc.sync, 3)
        load_tab(1)
        load_w(1)
        load_w(LAST)
        load_tab(LAST)
        nc.sync.dma_start(bias[:], b.rearrange("(p h) -> p h", h=HALVES))
        nc.sync.dma_start(offs2_sb[:], offs2)
        nc.sync.dma_start(wgo_sb[:], wgo)

        placed = [keep.tile([P, T], F32, name=f"placed{h}") for h in range(HALVES)]
        for h in range(HALVES):
            nc.vector.memset(placed[h][:], 0.0)

        words = {}
        scales = keep.tile([P, S], U8, name="scales", align_bytes=64)
        w_bf = [keep.tile([P, M, PACK], BF16, name=f"w_bf{a}", tag=f"w_bf{a}", align_bytes=64) for a in range(PASSES)]
        w_words = [keep.tile([P, M], U32, name=f"w_words{a}", align_bytes=64) for a in range(PASSES)]
        w_scales = [keep.tile([P, M], U8, name=f"w_scales{a}", align_bytes=64) for a in range(PASSES)]
        acc = [
            {first: psum.tile([P, end - first], F32, name=f"acc{h}_{first}") for spans in SPANS for first, end in spans}
            for h in range(HALVES)
        ]
        y = [
            [keep.tile([P, end - first], F32, name=f"y{h}{piece}") for piece, (first, end) in enumerate(PIECES)]
            for h in range(HALVES)
        ]

        def entries(list_tile, first, end):
            return list_tile[:, first // PER_COLUMN : end // PER_COLUMN]

        def new_words(a, tag):
            words[a] = keep.tile([P, S], U32, name=f"words{a}", tag=tag, align_bytes=64)

        def gather_words(a, first, end):
            nc.vector.tensor_copy(words[a][:, first:end], tab_words[a][:].bitcast(U32).indirect(entries(offs_sb, first, end)))

        def round_w(a):
            nc.scalar.copy(
                w_bf[a][:].rearrange("p (h c i) j -> p c j i h", h=HALVES, i=RUN // HALVES),
                w_raw[a][:].rearrange("p j (c i h) -> p c j i h", h=HALVES, i=RUN // HALVES),
            )

        def round_half(a, h):
            nc.scalar.copy(
                w_bf[a][:, P * h : P * (h + 1), :].rearrange("p (c i) j -> p c j i", i=RUN),
                w_raw[a][:].rearrange("p j (c i h) -> p h c j i", h=HALVES, i=RUN)[:, h],
            )

        def quantise_w(a, first, end):
            nc.vector.quantize_mx(
                w_words[a][:, first:end].bitcast(FP8X4),
                w_scales[a][:, first:end],
                w_bf[a][:, first:end, :].rearrange("p n j -> p (n j)"),
            )

        def multiply(h, piece, a):
            channels = slice(P * h, P * (h + 1))
            for first, end in SPANS[piece]:
                nc.tensor.matmul_mx(
                    acc[h][first][:],
                    lhsT=w_words[a][:, channels].bitcast(FP8X4),
                    lhsT_scale=w_scales[a][:, channels],
                    rhs=words[a][:, first:end].bitcast(FP8X4),
                    rhs_scale=scales[SCALE_ROWS * a : P, first:end],
                    start=(a == 0),
                    stop=(a == LAST),
                )

        def multiply_pass(a):
            for piece in range(len(PIECES)):
                for h in range(HALVES):
                    multiply(h, piece, a)

        new_words(0, "words0")
        gather_words(0, 0, S)
        nc.vector.tensor_copy(scales[:], tab_scales[:].bitcast(U8).indirect(offs_sb[:]))
        round_w(0)
        quantise_w(0, 0, M)
        new_words(1, "w_bf0")
        gather_words(1, 0, S)
        multiply_pass(0)
        for h in range(HALVES):
            round_half(1, h)
            quantise_w(1, P * h, P * (h + 1))
            for piece in range(len(PIECES)):
                multiply(h, piece, 1)

        for h in range(HALVES):
            round_half(LAST, h)
        quantise_w(LAST, 0, P)
        new_words(LAST, "words2")
        for piece, (first, end) in enumerate(PIECES):
            gather_words(LAST, first, end)
            if piece == 0:
                quantise_w(LAST, P, M)
            for h in range(HALVES):
                multiply(h, piece, LAST)

        for piece, (first, end) in enumerate(PIECES):
            for h in range(HALVES):
                for span_first, span_end in SPANS[piece]:
                    nc.scalar.activation(
                        y[h][piece][:, span_first - first : span_end - first],
                        acc[h][span_first][:],
                        IDENT,
                        bias=bias[:, h : h + 1],
                    )
                nc.vector.tensor_tensor(
                    placed[h][:].indirect(entries(offs2_sb, first, end)), y[h][piece][:], wgo_sb[:, first:end], MULT
                )
        for h in range(HALVES):
            nc.sync.dma_start(out.rearrange("(p h) t -> h p t", h=HALVES)[h], placed[h][:])
